import numpy as np
import ml_dtypes


def mxq(x, axis, fmt="e4m3"):
    dtype, down = {"e4m3": (ml_dtypes.float8_e4m3fn, 7), "e5m2": (ml_dtypes.float8_e5m2, 14)}[fmt]
    v = np.moveaxis(np.asarray(x, np.float32).astype(ml_dtypes.bfloat16).astype(np.float64), axis, -1)
    blocks = v.reshape(v.shape[:-1] + (-1, 32))
    amax = np.abs(blocks).max(-1, keepdims=True)
    byte = np.maximum(np.where(amax > 0, np.frexp(amax)[1] - 1 + 127, 0) - down, 1)
    scale = np.exp2(byte - 127.0)
    codes = (blocks / scale).astype(np.float32).astype(dtype).astype(np.float64)
    return np.moveaxis((codes * scale).reshape(v.shape), -1, axis)


WIDE = False


def mx_kscale(k):
    if not WIDE:
        return np.ones(k)
    levels = np.array([10, -10, 5, -5, 0])
    if k % 512:
        return np.exp2(np.random.permutation(np.resize(levels, k // 32))).repeat(32)
    a = np.empty((k // 512, 16))
    for p in range(k // 512):
        a[p, :8] = np.random.permutation(np.resize(levels, 8))
        for g in range(8):
            far = levels[np.abs(levels - a[p, g]) >= 10]
            a[p, g + 8] = far[np.random.randint(len(far))]
    return np.exp2(a.ravel()).repeat(32)


def f64(x):
    return np.asarray(x).astype(np.float64)


def striped(idx):
    return np.tile(idx.reshape(-1, 16).T, (8, 1)).astype(np.uint16)


def unstriped(offs):
    return offs[:16].T.reshape(-1).astype(np.int64)


def striped8(idx):
    return np.concatenate([x.reshape(-1, 16).T for x in idx]).astype(np.uint16)


def runs(offs, k):
    lists = np.stack([offs[16 * r : 16 * r + 16].T.reshape(-1) for r in range(8)]).astype(np.int64)
    return lists[np.arange(k) % 512 // 64]


def pack_weight(w):
    k, n = w.shape
    w = f64(np.asarray(w, np.float32).astype(ml_dtypes.bfloat16)).reshape(k // 32, 32, n)
    amax = np.abs(w).max(1)
    byte = np.clip(np.where(amax > 0, np.frexp(amax)[1] - 1 + 127 - 7, 1), 1, 254)
    scaled = (w * np.exp2(127.0 - byte)[:, None, :]).reshape(k, n).astype(np.float32)
    words = np.ascontiguousarray(scaled.reshape(k // 512, 128, 4, n).transpose(0, 1, 3, 2)).astype(ml_dtypes.float8_e4m3fn).view(np.uint8)
    return words, np.ascontiguousarray(byte.astype(np.uint8).reshape(k // 512, 16, n))


def unpack_weight(words, scales):
    g, p, n, _ = words.shape
    vals = np.ascontiguousarray(words).view(ml_dtypes.float8_e4m3fn).astype(np.float64) * np.repeat(np.exp2(scales.astype(np.float64) - 127.0), 8, axis=1)[..., None]
    return vals.transpose(0, 1, 3, 2).reshape(g * 512, n)


def sigmoid(v):
    return 1.0 / (1.0 + np.exp(-np.maximum(v, -700.0)))


K, T, S, H, W, G = 512, 2048, 256, 512, 128, 2048


def setup_inputs():
    n = np.random.standard_normal
    s = mx_kscale(K)[:, None]
    packed_xT = pack_weight(n((K, T)) * s)
    packed_dT = pack_weight(n((K, G)) / s)
    perm = np.random.permutation(S)
    return {
        "x_words": packed_xT[0],
        "x_scales": packed_xT[1],
        "w1": (n((K, H)) / np.sqrt(K) / s).astype(np.float32),
        "gs": (np.random.uniform(0.5, 1.5, (K, 1)) * s).astype(np.float32),
        "d_words": packed_dT[0],
        "d_scales": packed_dT[1],
        "sl": np.random.uniform(1.0, 2.0, (H, 1)).astype(np.float32),
        "th": (0.5 * n((H, 1))).astype(np.float32),
        "offs": striped8(np.random.randint(0, T, (8, S))),
        "n1": striped(perm[:W]),
        "n2": striped(perm[W:]),
        "n3": striped(np.random.permutation(S)),
        "k1": striped8(np.random.randint(0, G, (8, H))),
        "n4": striped8(np.stack([np.random.permutation(S) for _ in range(8)])),
        "n5": striped8(np.stack([np.random.permutation(S) for _ in range(8)])),
    }


def reference(x_words, x_scales, w1, gs, d_words, d_scales, sl, th, offs, n1, n2, n3, k1, n4, n5):
    d_k1 = unpack_weight(d_words, d_scales)[np.arange(K)[:, None], runs(k1, K)]
    xq = unpack_weight(x_words, x_scales)[np.arange(K)[:, None], runs(offs, K)]
    y = mxq(f64(w1), 0, "e4m3").T @ xq
    pa = y[:, unstriped(n1)]
    pb = y[:, unstriped(n2)]
    rb = pa - pb
    ds = np.zeros((H, S))
    ds[:, unstriped(n1)] = pb
    dt = ds.copy()
    dt[:, unstriped(n2)] = rb
    z = f64(gs) * (np.maximum(dt, 0.5 * dt[:, unstriped(n3)]))
    h = 0.0625 * ((d_k1.T @ mxq(z, 0, "e4m3")))
    st = h - (h[np.arange(H)[:, None], runs(n4, H)])
    sg = sigmoid(f64(sl) * (st[np.arange(H)[:, None], runs(n5, H)] - f64(th)))
    return h * sg

@@ -1,0 +1,216 @@
+from contextlib import ExitStack
+
+import concourse.mybir as mybir
+
+F32 = mybir.dt.float32
+BF16 = mybir.dt.bfloat16
+I32 = mybir.dt.int32
+U32 = mybir.dt.uint32
+U16 = mybir.dt.uint16
+U8 = mybir.dt.uint8
+FP8X4 = mybir.dt.float8_e4m3fn_x4
+ALU = mybir.AluOpType
+ACT = mybir.ActivationFunctionType
+
+P = 128
+PACK = 4
+TABLE = 2048
+S = 256
+H = 512
+W = 128
+HALF = S // 2
+CAST_SPLIT = 80
+
+FLOPS = 2 * 2 * 512 * H * S
+
+
+def tile_picked_hdenseswapdehq_none_p_kernel(
+    tc, x_words, x_scales, w1, gs, d_words, d_scales, sl, th, offs, n1, n2, n3, k1, n4, n5, out
+):
+    nc = tc.nc
+    with ExitStack() as ctx:
+        lists = ctx.enter_context(tc.tile_pool(name="lists", bufs=1))
+        keep = ctx.enter_context(tc.tile_pool(name="keep", bufs=1))
+        psum = ctx.enter_context(tc.psum_pool(name="psum", bufs=1))
+
+        def load_list(src, name):
+            t = lists.tile(list(src.shape), U16, name=name)
+            nc.sync.dma_start(t[:], src)
+            return t
+
+        def load_words(src, name, tag):
+            t = keep.tile([P, TABLE], U32, name=name, tag=tag)
+            nc.sync.dma_start(t[:].bitcast(I32), src[0].rearrange("p n r -> p (n r)").bitcast(I32))
+            return t
+
+        def load_scale_rows(src, name, clearer, queue):
+            t = keep.tile([P, TABLE], U8, name=name)
+            clearer.memset(t[:].bitcast(I32), 0)
+            queue.dma_start(t[0:P:8, :].bitcast(I32), src[0].bitcast(I32))
+            return t
+
+        def place_scale_rows(picked, name, queue):
+            plane = keep.tile(list(picked.shape), U8, name=name, align_bytes=64)
+            nc.vector.memset(plane[:].bitcast(I32), 0)
+            for s in range(4):
+                queue.dma_start(plane[s:P:32, :].bitcast(I32), picked[8 * s : P : 32, :].bitcast(I32))
+            return plane
+
+        def load_rows(src, name):
+            t = keep.tile([P, PACK], F32, name=name)
+            nc.gpsimd.dma_start(t[:], src.rearrange("(p t) o -> p (t o)", t=PACK))
+            return t
+
+        offs_t = load_list(offs, "offs_t")
+        n2_t = load_list(n2, "n2_t")
+        n1_t = load_list(n1, "n1_t")
+        n3_t = load_list(n3, "n3_t")
+        k1_t = load_list(k1, "k1_t")
+        xs_win = load_scale_rows(x_scales, "xs_win", nc.vector, nc.sync)
+        w_raw = keep.tile([P, PACK, H], F32, tag="w_raw_then_d_words")
+        nc.sync.dma_start(w_raw[:], w1.rearrange("(p j) c -> p j c", j=PACK))
+        xw_win = load_words(x_words, "xw_win", "xw_win")
+        n4_t = load_list(n4, "n4_t")
+        n5_t = load_list(n5, "n5_t")
+
+        xs_pick = keep.tile([P, S], U8)
+        nc.vector.tensor_copy(xs_pick[:], xs_win[:].indirect(offs_t[:]))
+        xs_plane = place_scale_rows(xs_pick, "xs_plane", nc.scalar)
+
+        gs_t = load_rows(gs, "gs_t")
+        sl_t = load_rows(sl, "sl_t")
+        th_t = load_rows(th, "th_t")
+        ds_win = load_scale_rows(d_scales, "ds_win", nc.gpsimd, nc.gpsimd)
+
+        w_bf = keep.tile([P, PACK * H], BF16, align_bytes=64)
+        w_dst = w_bf[:].rearrange("p (t m j) -> p m j t", t=PACK, j=PACK)
+        w_src = w_raw[:].rearrange("p j (m t) -> p m j t", t=PACK)
+        nc.vector.tensor_copy(w_dst[:, :CAST_SPLIT], w_src[:, :CAST_SPLIT])
+        nc.scalar.activation(w_dst[:, CAST_SPLIT:], w_src[:, CAST_SPLIT:], ACT.Copy)
+        dw_win = load_words(d_words, "dw_win", "w_raw_then_d_words")
+        w_codes = keep.tile([P, H], U32, align_bytes=64, tag="w_codes_then_ds_pick")
+        w_plane = keep.tile([P, H], U8, align_bytes=64)
+        nc.vector.quantize_mx(out=w_codes[:].bitcast(FP8X4), scales=w_plane[:], in_=w_bf[:])
+
+        xw_pick = keep.tile([P, S], U32, align_bytes=64)
+        nc.vector.tensor_copy(xw_pick[:], xw_win[:].indirect(offs_t[:]))
+        y = []
+        for t in range(PACK):
+            cols = slice(t * P, (t + 1) * P)
+            acc = psum.tile([P, S], F32, name="acc", tag="bank%d" % t)
+            nc.tensor.matmul_mx(
+                out=acc[:], lhsT=w_codes[:, cols].bitcast(FP8X4), lhsT_scale=w_plane[:, cols],
+                rhs=xw_pick[:].bitcast(FP8X4), rhs_scale=xs_plane[:], start=True, stop=True,
+            )
+            y_t = keep.tile([P, S], F32, name="y%d" % t)
+            if t == 0:
+                nc.scalar.copy(y_t[:], acc[:])
+            else:
+                nc.vector.tensor_copy(y_t[:], acc[:])
+            y.append(y_t)
+
+        h_win = [keep.tile([P, 2 * S], F32, name="h_win%d" % t) for t in range(PACK)]
+        st_win = [keep.tile([P, 2 * S], F32, name="st_win%d" % t) for t in range(PACK)]
+        pa = [h_win[t][:, S : S + W] for t in range(PACK)]
+        pb = [h_win[t][:, S + W : 2 * S] for t in range(PACK)]
+        far = [st_win[t][:, S : 2 * S] for t in range(PACK)]
+        rb = [keep.tile([P, W], F32, name="rb%d" % t) for t in range(PACK)]
+        dt = [keep.tile([P, S], F32, name="dt%d" % t) for t in range(PACK)]
+        big = [keep.tile([P, S], F32, name="big%d" % t) for t in range(PACK)]
+        z_bf = [keep.tile([P, HALF, PACK], BF16, name="z_bf%d" % u, align_bytes=64) for u in range(2)]
+
+        def fetch_pairs(t):
+            nc.scalar.activation(pb[t], y[t][:].indirect(n2_t[:]), ACT.Copy)
+            nc.scalar.activation(pa[t], y[t][:].indirect(n1_t[:]), ACT.Copy)
+            nc.vector.tensor_tensor(rb[t][:], pa[t], pb[t], ALU.subtract)
+
+        def put_pb(t):
+            nc.scalar.activation(dt[t][:].indirect(n1_t[:]), pb[t], ACT.Copy)
+
+        def put_rb(t):
+            nc.scalar.activation(dt[t][:].indirect(n2_t[:]), rb[t][:], ACT.Copy)
+
+        def make_z(t, u):
+            cols = slice(u * HALF, (u + 1) * HALF)
+            nc.scalar.activation(far[t][:, cols], dt[t][:].indirect(n3_t[:, u * 8 : (u + 1) * 8]), ACT.Copy)
+            nc.vector.scalar_tensor_tensor(big[t][:, cols], far[t][:, cols], 0.5, dt[t][:, cols], ALU.mult, ALU.max)
+            nc.vector.tensor_scalar(z_bf[u][:, :, t], big[t][:, cols], gs_t[:, t : t + 1], None, ALU.mult)
+
+        dw_pick = keep.tile([P, H], U32)
+        ds_pick = keep.tile([P, H], U8, align_bytes=64, tag="w_codes_then_ds_pick")
+        d_codes = keep.tile([P, H], U32, align_bytes=64)
+        ds_dealt = keep.tile([P, H], U8)
+
+        def pick_dictionary(win, pick, u):
+            nc.vector.tensor_copy(pick[:, u * S : (u + 1) * S], win[:].indirect(k1_t[:, u * 16 : (u + 1) * 16]))
+
+        def deal(dst, src):
+            nc.vector.tensor_copy(dst.rearrange("p (t m) -> p m t", t=PACK), src.rearrange("p (m t) -> p m t", t=PACK))
+
+        pick_dictionary(ds_win, ds_pick, 0)
+        pick_dictionary(ds_win, ds_pick, 1)
+        deal(ds_dealt[:], ds_pick[:])
+        ds_plane = place_scale_rows(ds_dealt, "ds_plane", nc.sync)
+        bias = keep.tile([P, PACK], F32)
+        neg_sl = keep.tile([P, PACK], F32)
+        nc.gpsimd.tensor_scalar(neg_sl[:], sl_t[:], -1.0, None, ALU.mult)
+        nc.gpsimd.tensor_tensor(bias[:], neg_sl[:], th_t[:], ALU.mult)
+
+        fetch_pairs(0)
+        for t in range(PACK):
+            put_pb(t)
+            if t > 0:
+                make_z(t - 1, 0)
+            if t + 1 < PACK:
+                fetch_pairs(t + 1)
+            put_rb(t)
+            if t < 2:
+                pick_dictionary(dw_win, dw_pick, t)
+            if t == 2:
+                deal(d_codes[:].bitcast(I32), dw_pick[:].bitcast(I32))
+
+        def second_product(u, accs):
+            z_codes = keep.tile([P, HALF], U32, name="z_codes%d" % u, align_bytes=64)
+            z_plane = keep.tile([P, HALF], U8, name="z_plane%d" % u, align_bytes=64)
+            nc.vector.quantize_mx(
+                out=z_codes[:].bitcast(FP8X4), scales=z_plane[:], in_=z_bf[u][:].rearrange("p s t -> p (s t)")
+            )
+            for t in range(PACK):
+                cols = slice(t * P, (t + 1) * P)
+                nc.tensor.matmul_mx(
+                    out=accs[t], lhsT=d_codes[:, cols].bitcast(FP8X4), lhsT_scale=ds_plane[:, cols],
+                    rhs=z_codes[:].bitcast(FP8X4), rhs_scale=z_plane[:], start=True, stop=True,
+                )
+            for t in range(PACK):
+                nc.vector.tensor_scalar(h_win[t][:, u * HALF : (u + 1) * HALF], accs[t], 0.0625, None, ALU.mult)
+
+        make_z(0, 1)
+        make_z(PACK - 1, 0)
+        first = psum.tile([P, PACK, HALF], F32, name="first")
+        second_product(0, [first[:, t, :] for t in range(PACK)])
+        for t in range(1, PACK):
+            make_z(t, 1)
+        last = [psum.tile([P, S], F32, name="acc", tag="bank%d" % t) for t in range(PACK)]
+        second_product(1, [last[t][:, :HALF] for t in range(PACK)])
+
+        out_rows = out.rearrange("(p t) s -> p t s", t=PACK)
+        other = [keep.tile([P, S], F32, name="other%d" % t) for t in range(PACK)]
+        sg = [keep.tile([P, S], F32, name="sg%d" % t) for t in range(PACK)]
+        res = [keep.tile([P, S], F32, name="res%d" % t) for t in range(PACK)]
+
+        def make_st(t):
+            nc.scalar.activation(other[t][:], h_win[t][:].indirect(n4_t[:]), ACT.Copy)
+            nc.vector.tensor_tensor(st_win[t][:, :S], h_win[t][:, :S], other[t][:], ALU.subtract)
+
+        def gate(t):
+            nc.scalar.activation(
+                sg[t][:], st_win[t][:].indirect(n5_t[:]), ACT.Sigmoid, bias=bias[:, t : t + 1], scale=sl_t[:, t : t + 1]
+            )
+            nc.vector.tensor_tensor(res[t][:], h_win[t][:, :S], sg[t][:], ALU.mult)
+            nc.sync.dma_start(out_rows[:, t, :], res[t][:])
+
+        make_st(0)
+        for t in range(PACK):
+            if t + 1 < PACK:
+                make_st(t + 1)
+            gate(t)

@@ -61,6 +61,10 @@ def tile_picked_hdenseswapdehq_none_p_kernel(
             nc.gpsimd.dma_start(t[:], src.rearrange("(p t) o -> p (t o)", t=PACK))
             return t
 
+        warm = keep.tile([P, 2], F32)
+        nc.gpsimd.memset(warm[:, 0:1], 0.0)
+        nc.scalar.activation(warm[:, 1:2], warm[:, 0:1], ACT.Sigmoid)
+
         offs_t = load_list(offs, "offs_t")
         n2_t = load_list(n2, "n2_t")
         n1_t = load_list(n1, "n1_t")

@@ -92,7 +92,7 @@ def tile_picked_hdenseswapdehq_none_p_kernel(
         nc.vector.tensor_copy(w_dst[:, :CAST_SPLIT], w_src[:, :CAST_SPLIT])
         nc.scalar.activation(w_dst[:, CAST_SPLIT:], w_src[:, CAST_SPLIT:], ACT.Copy)
         dw_win = load_words(d_words, "dw_win", "w_raw_then_d_words")
-        w_codes = keep.tile([P, H], U32, align_bytes=64, tag="w_codes_then_ds_pick")
+        w_codes = keep.tile([P, H], U32, align_bytes=64)
         w_plane = keep.tile([P, H], U8, align_bytes=64)
         nc.vector.quantize_mx(out=w_codes[:].bitcast(FP8X4), scales=w_plane[:], in_=w_bf[:])
 
@@ -106,7 +106,7 @@ def tile_picked_hdenseswapdehq_none_p_kernel(
                 out=acc[:], lhsT=w_codes[:, cols].bitcast(FP8X4), lhsT_scale=w_plane[:, cols],
                 rhs=xw_pick[:].bitcast(FP8X4), rhs_scale=xs_plane[:], start=True, stop=True,
             )
-            y_t = keep.tile([P, S], F32, name="y%d" % t)
+            y_t = keep.tile([P, S], F32, name="y%d" % t, tag="y%d" % t)
             if t == 0:
                 nc.scalar.copy(y_t[:], acc[:])
             else:
@@ -117,11 +117,10 @@ def tile_picked_hdenseswapdehq_none_p_kernel(
         st_win = [keep.tile([P, 2 * S], F32, name="st_win%d" % t) for t in range(PACK)]
         pa = [h_win[t][:, S : S + W] for t in range(PACK)]
         pb = [h_win[t][:, S + W : 2 * S] for t in range(PACK)]
-        far = [st_win[t][:, S : 2 * S] for t in range(PACK)]
+        other = [st_win[t][:, S : 2 * S] for t in range(PACK)]
         rb = [keep.tile([P, W], F32, name="rb%d" % t) for t in range(PACK)]
         dt = [keep.tile([P, S], F32, name="dt%d" % t) for t in range(PACK)]
-        big = [keep.tile([P, S], F32, name="big%d" % t) for t in range(PACK)]
-        z_bf = [keep.tile([P, HALF, PACK], BF16, name="z_bf%d" % u, align_bytes=64) for u in range(2)]
+        z_bf = [keep.tile([P, HALF, PACK], BF16, name="z_bf%d" % u, tag="z_bf%d" % u, align_bytes=64) for u in range(2)]
 
         def fetch_pairs(t):
             nc.scalar.activation(pb[t], y[t][:].indirect(n2_t[:]), ACT.Copy)
@@ -136,25 +135,31 @@ def tile_picked_hdenseswapdehq_none_p_kernel(
 
         def make_z(t, u):
             cols = slice(u * HALF, (u + 1) * HALF)
-            nc.scalar.activation(far[t][:, cols], dt[t][:].indirect(n3_t[:, u * 8 : (u + 1) * 8]), ACT.Copy)
-            nc.vector.scalar_tensor_tensor(big[t][:, cols], far[t][:, cols], 0.5, dt[t][:, cols], ALU.mult, ALU.max)
-            nc.vector.tensor_scalar(z_bf[u][:, :, t], big[t][:, cols], gs_t[:, t : t + 1], None, ALU.mult)
+            far = keep.tile([P, HALF], F32, name="far%d%d" % (t, u))
+            big = keep.tile([P, HALF], F32, name="big%d%d" % (t, u))
+            nc.scalar.activation(far[:], dt[t][:].indirect(n3_t[:, u * 8 : (u + 1) * 8]), ACT.Copy)
+            nc.vector.scalar_tensor_tensor(big[:], far[:], 0.5, dt[t][:, cols], ALU.mult, ALU.max)
+            nc.vector.tensor_scalar(z_bf[u][:, :, t], big[:], gs_t[:, t : t + 1], None, ALU.mult)
 
-        dw_pick = keep.tile([P, H], U32)
-        ds_pick = keep.tile([P, H], U8, align_bytes=64, tag="w_codes_then_ds_pick")
         d_codes = keep.tile([P, H], U32, align_bytes=64)
         ds_dealt = keep.tile([P, H], U8)
 
-        def pick_dictionary(win, pick, u):
-            nc.vector.tensor_copy(pick[:, u * S : (u + 1) * S], win[:].indirect(k1_t[:, u * 16 : (u + 1) * 16]))
+        def pick_dictionary_scales():
+            ds_pick = keep.tile([P, H], U8, tag="y0")
+            nc.vector.tensor_copy(ds_pick[:], ds_win[:].indirect(k1_t[:]))
+            nc.vector.tensor_copy(
+                ds_dealt[:].rearrange("p (t m) -> p m t", t=PACK), ds_pick[:].rearrange("p (m t) -> p m t", t=PACK)
+            )
+            return place_scale_rows(ds_dealt, "ds_plane", nc.sync)
 
-        def deal(dst, src):
-            nc.vector.tensor_copy(dst.rearrange("p (t m) -> p m t", t=PACK), src.rearrange("p (m t) -> p m t", t=PACK))
+        def pick_dictionary_words(u):
+            dw_pick = keep.tile([P, S], U32, name="dw_pick%d" % u, tag="y%d" % (u + 1))
+            nc.vector.tensor_copy(dw_pick[:], dw_win[:].indirect(k1_t[:, u * 16 : (u + 1) * 16]))
+            nc.vector.tensor_copy(
+                d_codes[:].bitcast(I32).rearrange("p (t m) -> p m t", t=PACK)[:, u * 64 : (u + 1) * 64, :],
+                dw_pick[:].bitcast(I32).rearrange("p (m t) -> p m t", t=PACK),
+            )
 
-        pick_dictionary(ds_win, ds_pick, 0)
-        pick_dictionary(ds_win, ds_pick, 1)
-        deal(ds_dealt[:], ds_pick[:])
-        ds_plane = place_scale_rows(ds_dealt, "ds_plane", nc.sync)
         bias = keep.tile([P, PACK], F32)
         neg_sl = keep.tile([P, PACK], F32)
         nc.gpsimd.tensor_scalar(neg_sl[:], sl_t[:], -1.0, None, ALU.mult)
@@ -165,56 +170,69 @@ def tile_picked_hdenseswapdehq_none_p_kernel(
             put_pb(t)
             if t > 0:
                 make_z(t - 1, 0)
+            if 0 < t < PACK - 1:
+                make_z(t - 1, 1)
             if t + 1 < PACK:
                 fetch_pairs(t + 1)
             put_rb(t)
-            if t < 2:
-                pick_dictionary(dw_win, dw_pick, t)
-            if t == 2:
-                deal(d_codes[:].bitcast(I32), dw_pick[:].bitcast(I32))
+            if t == 0:
+                ds_plane = pick_dictionary_scales()
+            elif t < 3:
+                pick_dictionary_words(t - 1)
 
-        def second_product(u, accs):
-            z_codes = keep.tile([P, HALF], U32, name="z_codes%d" % u, align_bytes=64)
-            z_plane = keep.tile([P, HALF], U8, name="z_plane%d" % u, align_bytes=64)
+        z_codes = keep.tile([P, S], U32, align_bytes=64)
+        z_plane = keep.tile([P, S], U8, align_bytes=64)
+
+        def quantise_z(u):
+            cols = slice(u * HALF, (u + 1) * HALF)
             nc.vector.quantize_mx(
-                out=z_codes[:].bitcast(FP8X4), scales=z_plane[:], in_=z_bf[u][:].rearrange("p s t -> p (s t)")
+                out=z_codes[:, cols].bitcast(FP8X4), scales=z_plane[:, cols], in_=z_bf[u][:].rearrange("p s t -> p (s t)")
             )
-            for t in range(PACK):
-                cols = slice(t * P, (t + 1) * P)
-                nc.tensor.matmul_mx(
-                    out=accs[t], lhsT=d_codes[:, cols].bitcast(FP8X4), lhsT_scale=ds_plane[:, cols],
-                    rhs=z_codes[:].bitcast(FP8X4), rhs_scale=z_plane[:], start=True, stop=True,
-                )
-            for t in range(PACK):
-                nc.vector.tensor_scalar(h_win[t][:, u * HALF : (u + 1) * HALF], accs[t], 0.0625, None, ALU.mult)
 
-        make_z(0, 1)
-        make_z(PACK - 1, 0)
-        first = psum.tile([P, PACK, HALF], F32, name="first")
-        second_product(0, [first[:, t, :] for t in range(PACK)])
+        def second_product(t, cols, tag):
+            acc = psum.tile([P, cols.stop - cols.start], F32, name="acc", tag=tag)
+            rows = slice(t * P, (t + 1) * P)
+            nc.tensor.matmul_mx(
+                out=acc[:], lhsT=d_codes[:, rows].bitcast(FP8X4), lhsT_scale=ds_plane[:, rows],
+                rhs=z_codes[:, cols].bitcast(FP8X4), rhs_scale=z_plane[:, cols], start=True, stop=True,
+            )
+            if t == 0:
+                nc.scalar.activation(h_win[t][:, cols], acc[:], ACT.Copy, scale=0.0625)
+            else:
+                nc.vector.tensor_scalar(h_win[t][:, cols], acc[:], 0.0625, None, ALU.mult)
+
+        make_z(2, 1)
+        make_z(3, 0)
+        quantise_z(0)
+        second_product(0, slice(0, HALF), "left")
+        make_z(3, 1)
+        quantise_z(1)
+        second_product(0, slice(HALF, S), "bank0")
         for t in range(1, PACK):
-            make_z(t, 1)
-        last = [psum.tile([P, S], F32, name="acc", tag="bank%d" % t) for t in range(PACK)]
-        second_product(1, [last[t][:, :HALF] for t in range(PACK)])
+            second_product(t, slice(0, S), "bank%d" % t)
 
         out_rows = out.rearrange("(p t) s -> p t s", t=PACK)
-        other = [keep.tile([P, S], F32, name="other%d" % t) for t in range(PACK)]
         sg = [keep.tile([P, S], F32, name="sg%d" % t) for t in range(PACK)]
         res = [keep.tile([P, S], F32, name="res%d" % t) for t in range(PACK)]
 
         def make_st(t):
-            nc.scalar.activation(other[t][:], h_win[t][:].indirect(n4_t[:]), ACT.Copy)
-            nc.vector.tensor_tensor(st_win[t][:, :S], h_win[t][:, :S], other[t][:], ALU.subtract)
+            nc.scalar.activation(other[t], h_win[t][:].indirect(n4_t[:]), ACT.Copy)
+            nc.vector.tensor_tensor(st_win[t][:, :S], h_win[t][:, :S], other[t], ALU.subtract)
 
-        def gate(t):
-            nc.scalar.activation(
-                sg[t][:], st_win[t][:].indirect(n5_t[:]), ACT.Sigmoid, bias=bias[:, t : t + 1], scale=sl_t[:, t : t + 1]
-            )
-            nc.vector.tensor_tensor(res[t][:], h_win[t][:, :S], sg[t][:], ALU.mult)
-            nc.sync.dma_start(out_rows[:, t, :], res[t][:])
+        def gate(t, pieces):
+            width = S // pieces
+            for u in range(pieces):
+                cols = slice(u * width, (u + 1) * width)
+                nc.scalar.activation(
+                    sg[t][:, cols], st_win[t][:].indirect(n5_t[:, u * width // 16 : (u + 1) * width // 16]),
+                    ACT.Sigmoid, bias=bias[:, t : t + 1], scale=sl_t[:, t : t + 1],
+                )
+                nc.vector.tensor_tensor(res[t][:, cols], h_win[t][:, cols], sg[t][:, cols], ALU.mult)
+                nc.sync.dma_start(out_rows[:, t, cols], res[t][:, cols])
 
         make_st(0)
+        make_st(1)
         for t in range(PACK):
-            if t + 1 < PACK:
-                make_st(t + 1)
-            gate(t)
+            if t + 2 < PACK:
+                make_st(t + 2)
+            gate(t, 2 if t == PACK - 1 else 1)

from contextlib import ExitStack

import concourse.mybir as mybir

F32 = mybir.dt.float32
BF16 = mybir.dt.bfloat16
I32 = mybir.dt.int32
U32 = mybir.dt.uint32
U16 = mybir.dt.uint16
U8 = mybir.dt.uint8
FP8X4 = mybir.dt.float8_e4m3fn_x4
ALU = mybir.AluOpType
ACT = mybir.ActivationFunctionType

P = 128
PACK = 4
TABLE = 2048
S = 256
H = 512
W = 128
HALF = S // 2
CAST_SPLIT = 80

FLOPS = 2 * 2 * 512 * H * S


def tile_picked_hdenseswapdehq_none_p_kernel(
    tc, x_words, x_scales, w1, gs, d_words, d_scales, sl, th, offs, n1, n2, n3, k1, n4, n5, out
):
    nc = tc.nc
    with ExitStack() as ctx:
        lists = ctx.enter_context(tc.tile_pool(name="lists", bufs=1))
        keep = ctx.enter_context(tc.tile_pool(name="keep", bufs=1))
        psum = ctx.enter_context(tc.psum_pool(name="psum", bufs=1))

        def load_list(src, name):
            t = lists.tile(list(src.shape), U16, name=name)
            nc.sync.dma_start(t[:], src)
            return t

        def load_words(src, name, tag):
            t = keep.tile([P, TABLE], U32, name=name, tag=tag)
            nc.sync.dma_start(t[:].bitcast(I32), src[0].rearrange("p n r -> p (n r)").bitcast(I32))
            return t

        def load_scale_rows(src, name, clearer, queue):
            t = keep.tile([P, TABLE], U8, name=name)
            clearer.memset(t[:].bitcast(I32), 0)
            queue.dma_start(t[0:P:8, :].bitcast(I32), src[0].bitcast(I32))
            return t

        def place_scale_rows(picked, name, queue):
            plane = keep.tile(list(picked.shape), U8, name=name, align_bytes=64)
            nc.vector.memset(plane[:].bitcast(I32), 0)
            for s in range(4):
                queue.dma_start(plane[s:P:32, :].bitcast(I32), picked[8 * s : P : 32, :].bitcast(I32))
            return plane

        def load_rows(src, name):
            t = keep.tile([P, PACK], F32, name=name)
            nc.gpsimd.dma_start(t[:], src.rearrange("(p t) o -> p (t o)", t=PACK))
            return t

        warm = keep.tile([P, 2], F32)
        nc.gpsimd.memset(warm[:, 0:1], 0.0)
        nc.scalar.activation(warm[:, 1:2], warm[:, 0:1], ACT.Sigmoid)

        offs_t = load_list(offs, "offs_t")
        n2_t = load_list(n2, "n2_t")
        n1_t = load_list(n1, "n1_t")
        n3_t = load_list(n3, "n3_t")
        k1_t = load_list(k1, "k1_t")
        xs_win = load_scale_rows(x_scales, "xs_win", nc.vector, nc.sync)
        w_raw = keep.tile([P, PACK, H], F32, tag="w_raw_then_d_words")
        nc.sync.dma_start(w_raw[:], w1.rearrange("(p j) c -> p j c", j=PACK))
        xw_win = load_words(x_words, "xw_win", "xw_win")
        n4_t = load_list(n4, "n4_t")
        n5_t = load_list(n5, "n5_t")

        xs_pick = keep.tile([P, S], U8)
        nc.vector.tensor_copy(xs_pick[:], xs_win[:].indirect(offs_t[:]))
        xs_plane = place_scale_rows(xs_pick, "xs_plane", nc.scalar)

        gs_t = load_rows(gs, "gs_t")
        sl_t = load_rows(sl, "sl_t")
        th_t = load_rows(th, "th_t")
        ds_win = load_scale_rows(d_scales, "ds_win", nc.gpsimd, nc.gpsimd)

        w_bf = keep.tile([P, PACK * H], BF16, align_bytes=64)
        w_dst = w_bf[:].rearrange("p (t m j) -> p m j t", t=PACK, j=PACK)
        w_src = w_raw[:].rearrange("p j (m t) -> p m j t", t=PACK)
        nc.vector.tensor_copy(w_dst[:, :CAST_SPLIT], w_src[:, :CAST_SPLIT])
        nc.scalar.activation(w_dst[:, CAST_SPLIT:], w_src[:, CAST_SPLIT:], ACT.Copy)
        dw_win = load_words(d_words, "dw_win", "w_raw_then_d_words")
        w_codes = keep.tile([P, H], U32, align_bytes=64)
        w_plane = keep.tile([P, H], U8, align_bytes=64)
        nc.vector.quantize_mx(out=w_codes[:].bitcast(FP8X4), scales=w_plane[:], in_=w_bf[:])

        xw_pick = keep.tile([P, S], U32, align_bytes=64)
        nc.vector.tensor_copy(xw_pick[:], xw_win[:].indirect(offs_t[:]))
        y = []
        for t in range(PACK):
            cols = slice(t * P, (t + 1) * P)
            acc = psum.tile([P, S], F32, name="acc", tag="bank%d" % t)
            nc.tensor.matmul_mx(
                out=acc[:], lhsT=w_codes[:, cols].bitcast(FP8X4), lhsT_scale=w_plane[:, cols],
                rhs=xw_pick[:].bitcast(FP8X4), rhs_scale=xs_plane[:], start=True, stop=True,
            )
            y_t = keep.tile([P, S], F32, name="y%d" % t, tag="y%d" % t)
            if t == 0:
                nc.scalar.copy(y_t[:], acc[:])
            else:
                nc.vector.tensor_copy(y_t[:], acc[:])
            y.append(y_t)

        h_win = [keep.tile([P, 2 * S], F32, name="h_win%d" % t) for t in range(PACK)]
        st_win = [keep.tile([P, 2 * S], F32, name="st_win%d" % t) for t in range(PACK)]
        pa = [h_win[t][:, S : S + W] for t in range(PACK)]
        pb = [h_win[t][:, S + W : 2 * S] for t in range(PACK)]
        other = [st_win[t][:, S : 2 * S] for t in range(PACK)]
        rb = [keep.tile([P, W], F32, name="rb%d" % t) for t in range(PACK)]
        dt = [keep.tile([P, S], F32, name="dt%d" % t) for t in range(PACK)]
        z_bf = [keep.tile([P, HALF, PACK], BF16, name="z_bf%d" % u, tag="z_bf%d" % u, align_bytes=64) for u in range(2)]

        def fetch_pairs(t):
            nc.scalar.activation(pb[t], y[t][:].indirect(n2_t[:]), ACT.Copy)
            nc.scalar.activation(pa[t], y[t][:].indirect(n1_t[:]), ACT.Copy)
            nc.vector.tensor_tensor(rb[t][:], pa[t], pb[t], ALU.subtract)

        def put_pb(t):
            nc.scalar.activation(dt[t][:].indirect(n1_t[:]), pb[t], ACT.Copy)

        def put_rb(t):
            nc.scalar.activation(dt[t][:].indirect(n2_t[:]), rb[t][:], ACT.Copy)

        def make_z(t, u):
            cols = slice(u * HALF, (u + 1) * HALF)
            far = keep.tile([P, HALF], F32, name="far%d%d" % (t, u))
            big = keep.tile([P, HALF], F32, name="big%d%d" % (t, u))
            nc.scalar.activation(far[:], dt[t][:].indirect(n3_t[:, u * 8 : (u + 1) * 8]), ACT.Copy)
            nc.vector.scalar_tensor_tensor(big[:], far[:], 0.5, dt[t][:, cols], ALU.mult, ALU.max)
            nc.vector.tensor_scalar(z_bf[u][:, :, t], big[:], gs_t[:, t : t + 1], None, ALU.mult)

        d_codes = keep.tile([P, H], U32, align_bytes=64)
        ds_dealt = keep.tile([P, H], U8)

        def pick_dictionary_scales():
            ds_pick = keep.tile([P, H], U8, tag="y0")
            nc.vector.tensor_copy(ds_pick[:], ds_win[:].indirect(k1_t[:]))
            nc.vector.tensor_copy(
                ds_dealt[:].rearrange("p (t m) -> p m t", t=PACK), ds_pick[:].rearrange("p (m t) -> p m t", t=PACK)
            )
            return place_scale_rows(ds_dealt, "ds_plane", nc.sync)

        def pick_dictionary_words(u):
            dw_pick = keep.tile([P, S], U32, name="dw_pick%d" % u, tag="y%d" % (u + 1))
            nc.vector.tensor_copy(dw_pick[:], dw_win[:].indirect(k1_t[:, u * 16 : (u + 1) * 16]))
            nc.vector.tensor_copy(
                d_codes[:].bitcast(I32).rearrange("p (t m) -> p m t", t=PACK)[:, u * 64 : (u + 1) * 64, :],
                dw_pick[:].bitcast(I32).rearrange("p (m t) -> p m t", t=PACK),
            )

        bias = keep.tile([P, PACK], F32)
        neg_sl = keep.tile([P, PACK], F32)
        nc.gpsimd.tensor_scalar(neg_sl[:], sl_t[:], -1.0, None, ALU.mult)
        nc.gpsimd.tensor_tensor(bias[:], neg_sl[:], th_t[:], ALU.mult)

        fetch_pairs(0)
        for t in range(PACK):
            put_pb(t)
            if t > 0:
                make_z(t - 1, 0)
            if 0 < t < PACK - 1:
                make_z(t - 1, 1)
            if t + 1 < PACK:
                fetch_pairs(t + 1)
            put_rb(t)
            if t == 0:
                ds_plane = pick_dictionary_scales()
            elif t < 3:
                pick_dictionary_words(t - 1)

        z_codes = keep.tile([P, S], U32, align_bytes=64)
        z_plane = keep.tile([P, S], U8, align_bytes=64)

        def quantise_z(u):
            cols = slice(u * HALF, (u + 1) * HALF)
            nc.vector.quantize_mx(
                out=z_codes[:, cols].bitcast(FP8X4), scales=z_plane[:, cols], in_=z_bf[u][:].rearrange("p s t -> p (s t)")
            )

        def second_product(t, cols, tag):
            acc = psum.tile([P, cols.stop - cols.start], F32, name="acc", tag=tag)
            rows = slice(t * P, (t + 1) * P)
            nc.tensor.matmul_mx(
                out=acc[:], lhsT=d_codes[:, rows].bitcast(FP8X4), lhsT_scale=ds_plane[:, rows],
                rhs=z_codes[:, cols].bitcast(FP8X4), rhs_scale=z_plane[:, cols], start=True, stop=True,
            )
            if t == 0:
                nc.scalar.activation(h_win[t][:, cols], acc[:], ACT.Copy, scale=0.0625)
            else:
                nc.vector.tensor_scalar(h_win[t][:, cols], acc[:], 0.0625, None, ALU.mult)

        make_z(2, 1)
        make_z(3, 0)
        quantise_z(0)
        second_product(0, slice(0, HALF), "left")
        make_z(3, 1)
        quantise_z(1)
        second_product(0, slice(HALF, S), "bank0")
        for t in range(1, PACK):
            second_product(t, slice(0, S), "bank%d" % t)

        out_rows = out.rearrange("(p t) s -> p t s", t=PACK)
        sg = [keep.tile([P, S], F32, name="sg%d" % t) for t in range(PACK)]
        res = [keep.tile([P, S], F32, name="res%d" % t) for t in range(PACK)]

        def make_st(t):
            nc.scalar.activation(other[t], h_win[t][:].indirect(n4_t[:]), ACT.Copy)
            nc.vector.tensor_tensor(st_win[t][:, :S], h_win[t][:, :S], other[t], ALU.subtract)

        def gate(t, pieces):
            width = S // pieces
            for u in range(pieces):
                cols = slice(u * width, (u + 1) * width)
                nc.scalar.activation(
                    sg[t][:, cols], st_win[t][:].indirect(n5_t[:, u * width // 16 : (u + 1) * width // 16]),
                    ACT.Sigmoid, bias=bias[:, t : t + 1], scale=sl_t[:, t : t + 1],
                )
                nc.vector.tensor_tensor(res[t][:, cols], h_win[t][:, cols], sg[t][:, cols], ALU.mult)
                nc.sync.dma_start(out_rows[:, t, cols], res[t][:, cols])

        make_st(0)
        make_st(1)
        for t in range(PACK):
            if t + 2 < PACK:
                make_st(t + 2)
            gate(t, 2 if t == PACK - 1 else 1)
